import numpy as np
import ml_dtypes


def mxq(x, axis, fmt="e4m3"):
    dtype, down = {"e4m3": (ml_dtypes.float8_e4m3fn, 7), "e5m2": (ml_dtypes.float8_e5m2, 14)}[fmt]
    v = np.moveaxis(np.asarray(x, np.float32).astype(ml_dtypes.bfloat16).astype(np.float64), axis, -1)
    blocks = v.reshape(v.shape[:-1] + (-1, 32))
    amax = np.abs(blocks).max(-1, keepdims=True)
    byte = np.maximum(np.where(amax > 0, np.frexp(amax)[1] - 1 + 127, 0) - down, 1)
    scale = np.exp2(byte - 127.0)
    codes = (blocks / scale).astype(np.float32).astype(dtype).astype(np.float64)
    return np.moveaxis((codes * scale).reshape(v.shape), -1, axis)


WIDE = False


def mx_kscale(k):
    if not WIDE:
        return np.ones(k)
    levels = np.array([10, -10, 5, -5, 0])
    if k % 512:
        return np.exp2(np.random.permutation(np.resize(levels, k // 32))).repeat(32)
    a = np.empty((k // 512, 16))
    for p in range(k // 512):
        a[p, :8] = np.random.permutation(np.resize(levels, 8))
        for g in range(8):
            far = levels[np.abs(levels - a[p, g]) >= 10]
            a[p, g + 8] = far[np.random.randint(len(far))]
    return np.exp2(a.ravel()).repeat(32)


def f64(x):
    return np.asarray(x).astype(np.float64)


def striped(idx):
    return np.tile(idx.reshape(-1, 16).T, (8, 1)).astype(np.uint16)


def unstriped(offs):
    return offs[:16].T.reshape(-1).astype(np.int64)


def relu(v):
    return np.maximum(v, 0.0)


K, T, E, C, N = 1536, 512, 6, 128, 512
TOP = 3
PAD = 64


def by_expert(wq, xq):
    return np.concatenate([wq[e].T @ xq[:, e * C:(e + 1) * C] for e in range(E)], axis=1)


def setup_inputs():
    n = np.random.standard_normal
    s = mx_kscale(K)[:, None]
    slot_token = np.empty(E * C, np.int64); pos = np.tile(E * C + np.arange(T) % PAD, (TOP, 1)); taken = np.zeros(T, np.int64)
    liked = np.random.randn(T)
    for e in np.random.permutation(E):
        free = np.flatnonzero(taken < TOP); pick = np.random.permutation(free[np.argsort(-(liked[free] + np.random.gumbel(size=free.size)))[:C]]); slot_token[e * C:(e + 1) * C] = pick
        pos[taken[pick], pick] = e * C + np.arange(C); taken[pick] += 1
    g = np.random.uniform(0.2, 0.8, (TOP, T))
    return {
        "xT": (n((K, T)) * s).astype(np.float32),
        "w": (n((E, K, N)) / np.sqrt(K) / s[None]).astype(np.float32),
        "b": (0.3 * n((N, E))).astype(np.float32),
        "gate": np.stack([np.tile(r, (N, 1)) for r in g]).astype(np.float32),
        "offs": striped(slot_token),
        "pos1": striped(pos[0]),
        "pos2": striped(pos[1]),
        "pos3": striped(pos[2]),
    }


def reference(xT, w, b, gate, offs, pos1, pos2, pos3):
    idx = unstriped(offs)
    xq = mxq(f64(xT)[:, idx], 0, "e4m3")
    y = by_expert(mxq(f64(w), 1, "e4m3"), xq)
    y = relu(y + np.repeat(f64(b), C, axis=1))
    y = np.concatenate([y, np.zeros((N, PAD))], axis=1)
    return sum(f64(gate[r]) * y[:, unstriped(p)] for r, p in enumerate((pos1, pos2, pos3)))

@@ -1,0 +1,184 @@
+from contextlib import ExitStack
+
+import concourse.mybir as mybir
+from concourse.masks import make_identity
+
+K, T, E, C, N = 1536, 512, 6, 128, 512
+TOP = 3
+PAD = 64
+SLOTS = E * C
+FLOPS = 2 * K * N * SLOTS
+BYTES = 4 * (K * T + E * K * N + N * E + TOP * T + N * T) + 2 * (SLOTS + TOP * T)
+
+F32 = mybir.dt.float32
+BF16 = mybir.dt.bfloat16
+U32 = mybir.dt.uint32
+I32 = mybir.dt.int32
+U16 = mybir.dt.uint16
+U8 = mybir.dt.uint8
+FP8X4 = mybir.dt.float8_e4m3fn_x4
+MULT = mybir.AluOpType.mult
+ADD = mybir.AluOpType.add
+RELU = mybir.ActivationFunctionType.Relu
+
+P = 128
+PACK = 4
+PASSES = K // (P * PACK)
+UNITS = E * PASSES
+BLOCKS = N // P
+GROUP = 6
+HALF = SLOTS // 2
+FINE = 3
+
+
+def tile_moe_ecr_lin_relu_kernel(tc, xT, w, b, gate, offs, pos1, pos2, pos3, out):
+    nc = tc.nc
+    with ExitStack() as ctx:
+        keep = ctx.enter_context(tc.tile_pool(name="keep", bufs=1))
+        rawp = ctx.enter_context(tc.tile_pool(name="rawp", bufs=1))
+        xp = ctx.enter_context(tc.tile_pool(name="xp", bufs=PASSES))
+        bfp = ctx.enter_context(tc.tile_pool(name="bfp", bufs=7))
+        codep = ctx.enter_context(tc.tile_pool(name="codep", bufs=6))
+        prodp = ctx.enter_context(tc.tile_pool(name="prodp", bufs=1))
+        psum = ctx.enter_context(tc.psum_pool(name="psum", bufs=8))
+
+        x_view = xT.rearrange("(a p j) t -> a p j t", p=P, j=PACK)
+        w_view = w.rearrange("e k n -> (e k) n").rearrange("(u p j) n -> p j u n", p=P, j=PACK)
+
+        offs_t = keep.tile([P, SLOTS // 16], U16, name="offs_t")
+        pos_t = [keep.tile([P, T // 16], U16, name="pos_t%d" % r) for r in range(TOP)]
+        gate_t = keep.tile([P, TOP, T], F32, name="gate_t")
+        bias_t = keep.tile([P, BLOCKS, E], F32, name="bias_t")
+        x_words = [keep.tile([P, T], U32, name="x_words%d" % a, align_bytes=64) for a in range(PASSES)]
+        x_scales = keep.tile([P, T], U8, name="x_scales", align_bytes=64)
+        s_words = [keep.tile([P, SLOTS], U32, name="s_words%d" % a, align_bytes=64) for a in range(PASSES)]
+        s_scales = keep.tile([P, SLOTS], U8, name="s_scales", align_bytes=64)
+
+        def cast(on_vector, raw, c0, width):
+            grouped = bfp.tile([P, width * PACK], BF16, name="grouped", tag="grouped", align_bytes=64)
+            dst = grouped[:].rearrange("p (c i t) -> p c t i", i=4, t=PACK)
+            src = raw[:, :, c0:c0 + width].rearrange("p t (c i) -> p c t i", i=4)
+            if on_vector:
+                nc.vector.tensor_copy(out=dst, in_=src)
+            else:
+                nc.scalar.copy(out=dst, in_=src)
+            return grouped
+
+        ident = keep.tile([P, P], F32, name="ident")
+        make_identity(nc, ident[:])
+        gate_rows = bfp.tile([P, TOP, P], F32, name="gate_rows", tag="grouped", align_bytes=64)
+        nc.vector.memset(gate_rows[:], 0.0)
+
+        x_raw = []
+        for a in range(PASSES):
+            raw = xp.tile([P, PACK, T], F32, name="xraw", tag="xraw")
+            nc.sync.dma_start(out=raw[:], in_=x_view[a])
+            x_raw.append(raw)
+            if a == 0:
+                nc.sync.dma_start(offs_t[:], offs)
+                nc.sync.dma_start(out=gate_rows[0:T // P], in_=gate[:, 0, :].rearrange("r (q t) -> q r t", t=P))
+
+        w_raw = {}
+        fine = []
+
+        def load_group(blk, u0, units):
+            cols = slice(blk * P, (blk + 1) * P)
+            if units == 1:
+                if u0 % FINE == 0:
+                    fine.append(xp.tile([P, FINE, PACK, P], F32, name="xraw", tag="xraw"))
+                raw = fine[-1][:, u0 % FINE]
+                nc.sync.dma_start(out=raw, in_=w_view[:, :, u0, cols])
+            else:
+                raw = rawp.tile([P, PACK, units * P], F32, name="raw", tag="raw%d_%d" % (blk, u0))
+                for j in range(PACK):
+                    nc.sync.dma_start(out=raw[:, j, :].rearrange("p (u n) -> p u n", n=P), in_=w_view[:, j, u0:u0 + units, cols])
+            w_raw[(blk, u0)] = raw
+
+        def groups_of(blk):
+            if blk == BLOCKS - 1:
+                return [(0, GROUP), (GROUP, GROUP)] + [(u, 1) for u in range(2 * GROUP, UNITS)]
+            return [(u, GROUP) for u in range(0, UNITS, GROUP)]
+
+        for blk in range(BLOCKS):
+            for u0, units in groups_of(blk):
+                load_group(blk, u0, units)
+                if blk == 0 and u0 == 0:
+                    nc.sync.dma_start(out=bias_t[:], in_=b.rearrange("(c p) e -> p c e", p=P))
+            if blk == 0:
+                for r, pos in enumerate((pos1, pos2, pos3)):
+                    nc.sync.dma_start(pos_t[r][:], pos)
+
+        nc.vector.memset(x_scales[:].bitcast(I32), 0)
+        out_t = xp.tile([P, BLOCKS, T], F32, name="xraw", tag="xraw")
+        for a in range(PASSES):
+            for h in range(2):
+                cols = slice(h * (T // 2), (h + 1) * (T // 2))
+                grouped = cast(a == 0 and h == 0, x_raw[a], h * (T // 2), T // 2)
+                nc.vector.quantize_mx(out=x_words[a][:, cols].bitcast(FP8X4), scales=x_scales[4 * a:P, cols], in_=grouped[:])
+            for h in range(2):
+                nc.vector.tensor_copy(s_words[a][:, h * HALF:(h + 1) * HALF],
+                                      x_words[a][:].indirect(offs_t[:, h * (HALF // 16):(h + 1) * (HALF // 16)]))
+        for h in range(2):
+            nc.vector.tensor_copy(s_scales[:, h * HALF:(h + 1) * HALF],
+                                  x_scales[:].indirect(offs_t[:, h * (HALF // 16):(h + 1) * (HALF // 16)]))
+
+        turned = psum.tile([P, TOP, P], F32, name="acc")
+        for r in range(TOP):
+            nc.tensor.transpose(turned[:, r, :], gate_rows[:, r, :], ident[:])
+        gate_cols = keep.tile([P, TOP, T // P], F32, name="gate_cols")
+        nc.scalar.copy(out=gate_cols[:], in_=turned[:, :, 0:T // P])
+        for r in range(TOP):
+            spread = psum.tile([P, T], F32, name="acc")
+            for q in range(T // P):
+                nc.tensor.transpose(spread[:, q * P:(q + 1) * P], gate_cols[:, r, q:q + 1].to_broadcast([P, P]), ident[:])
+            nc.scalar.copy(out=gate_t[:, r, :], in_=spread[:])
+
+        def chunks_of(blk, u0, units):
+            if units == 1:
+                return [(u0, 1, False)]
+            return [(u0, 4, False), (u0 + 4, 2, u0 < 2 * GROUP)]
+
+        def experts(blk):
+            codes = {}
+            done = 0
+            sums = []
+            for u0, units in groups_of(blk):
+                for c0, cu, on_vector in chunks_of(blk, u0, units):
+                    grouped = cast(on_vector, w_raw[(blk, u0)], (c0 - u0) * P, cu * P)
+                    words = codep.tile([P, cu * P], U32, name="words", tag="words", align_bytes=64)
+                    scales = codep.tile([P, cu * P], U8, name="scales", tag="scales", align_bytes=64)
+                    nc.vector.quantize_mx(out=words[:].bitcast(FP8X4), scales=scales[:], in_=grouped[:])
+                    for u in range(c0, c0 + cu):
+                        codes[u] = (words, scales, slice((u - c0) * P, (u - c0 + 1) * P))
+                    while (done + 1) * PASSES <= c0 + cu:
+                        e = done
+                        slots = slice(e * C, (e + 1) * C)
+                        acc = psum.tile([P, C], F32, name="acc")
+                        for a in range(PASSES):
+                            wd, sc, cols = codes[e * PASSES + a]
+                            nc.tensor.matmul_mx(out=acc[:], lhsT=wd[:, cols].bitcast(FP8X4), lhsT_scale=sc[:, cols],
+                                                rhs=s_words[a][:, slots].bitcast(FP8X4), rhs_scale=s_scales[4 * a:P, slots],
+                                                start=(a == 0), stop=(a == PASSES - 1))
+                        sums.append(acc)
+                        done = done + 1
+            last = GROUP if blk == BLOCKS - 1 else 2 * GROUP
+            y = rawp.tile([P, SLOTS + PAD], F32, name="y", tag="raw%d_%d" % (blk, last))
+            nc.gpsimd.memset(y[:, SLOTS:], 0.0)
+            for e in range(E):
+                nc.scalar.activation(y[:, e * C:(e + 1) * C], sums[e][:], RELU, bias=bias_t[:, blk, e:e + 1])
+            return y
+
+        def combine(blk, y, pieces):
+            width = T // pieces
+            prods = [prodp.tile([P, T], F32, name="prod", tag="prod%d" % r) for r in range(TOP)]
+            for h in range(pieces):
+                toks = slice(h * width, (h + 1) * width)
+                for r in range(TOP):
+                    nc.vector.tensor_tensor(prods[r][:, toks], y[:].indirect(pos_t[r][:, toks.start // 16:toks.stop // 16]),
+                                            gate_t[:, r, toks], MULT)
+                nc.vector.tensor_tensor(prods[0][:, toks], prods[0][:, toks], prods[1][:, toks], ADD)
+                nc.vector.tensor_tensor(out_t[:, blk, toks], prods[0][:, toks], prods[2][:, toks], ADD)
+                nc.sync.dma_start(out=out[blk * P:(blk + 1) * P, toks], in_=out_t[:, blk, toks])
+
+        for blk in range(BLOCKS):
+            combine(blk, experts(blk), 2 if blk == BLOCKS - 1 else 1)

@@ -24,11 +24,10 @@ RELU = mybir.ActivationFunctionType.Relu
 P = 128
 PACK = 4
 PASSES = K // (P * PACK)
-UNITS = E * PASSES
 BLOCKS = N // P
-GROUP = 6
 HALF = SLOTS // 2
-FINE = 3
+EARLY = 4
+VECTOR_FROM = 2
 
 
 def tile_moe_ecr_lin_relu_kernel(tc, xT, w, b, gate, offs, pos1, pos2, pos3, out):
@@ -36,14 +35,13 @@ def tile_moe_ecr_lin_relu_kernel(tc, xT, w, b, gate, offs, pos1, pos2, pos3, out
     with ExitStack() as ctx:
         keep = ctx.enter_context(tc.tile_pool(name="keep", bufs=1))
         rawp = ctx.enter_context(tc.tile_pool(name="rawp", bufs=1))
-        xp = ctx.enter_context(tc.tile_pool(name="xp", bufs=PASSES))
-        bfp = ctx.enter_context(tc.tile_pool(name="bfp", bufs=7))
-        codep = ctx.enter_context(tc.tile_pool(name="codep", bufs=6))
-        prodp = ctx.enter_context(tc.tile_pool(name="prodp", bufs=1))
+        bfp = ctx.enter_context(tc.tile_pool(name="bfp", bufs=8))
+        lastp = ctx.enter_context(tc.tile_pool(name="lastp", bufs=1))
+        codep = ctx.enter_context(tc.tile_pool(name="codep", bufs=12))
         psum = ctx.enter_context(tc.psum_pool(name="psum", bufs=8))
 
         x_view = xT.rearrange("(a p j) t -> a p j t", p=P, j=PACK)
-        w_view = w.rearrange("e k n -> (e k) n").rearrange("(u p j) n -> p j u n", p=P, j=PACK)
+        w_view = w.rearrange("e (a p j) n -> e a p j n", p=P, j=PACK)
 
         offs_t = keep.tile([P, SLOTS // 16], U16, name="offs_t")
         pos_t = [keep.tile([P, T // 16], U16, name="pos_t%d" % r) for r in range(TOP)]
@@ -53,9 +51,13 @@ def tile_moe_ecr_lin_relu_kernel(tc, xT, w, b, gate, offs, pos1, pos2, pos3, out
         x_scales = keep.tile([P, T], U8, name="x_scales", align_bytes=64)
         s_words = [keep.tile([P, SLOTS], U32, name="s_words%d" % a, align_bytes=64) for a in range(PASSES)]
         s_scales = keep.tile([P, SLOTS], U8, name="s_scales", align_bytes=64)
+        ident = keep.tile([P, P], F32, name="ident")
+        make_identity(nc, ident[:])
+        gate_rows = bfp.tile([P, TOP, P], F32, name="gate_rows", tag="grouped", align_bytes=64)
+        nc.vector.memset(gate_rows[:], 0.0)
 
-        def cast(on_vector, raw, c0, width):
-            grouped = bfp.tile([P, width * PACK], BF16, name="grouped", tag="grouped", align_bytes=64)
+        def cast(on_vector, raw, c0, width, pool):
+            grouped = pool.tile([P, width * PACK], BF16, name="grouped", tag="grouped", align_bytes=64)
             dst = grouped[:].rearrange("p (c i t) -> p c t i", i=4, t=PACK)
             src = raw[:, :, c0:c0 + width].rearrange("p t (c i) -> p c t i", i=4)
             if on_vector:
@@ -64,56 +66,56 @@ def tile_moe_ecr_lin_relu_kernel(tc, xT, w, b, gate, offs, pos1, pos2, pos3, out
                 nc.scalar.copy(out=dst, in_=src)
             return grouped
 
-        ident = keep.tile([P, P], F32, name="ident")
-        make_identity(nc, ident[:])
-        gate_rows = bfp.tile([P, TOP, P], F32, name="gate_rows", tag="grouped", align_bytes=64)
-        nc.vector.memset(gate_rows[:], 0.0)
+        def quantise(grouped, width):
+            words = codep.tile([P, width], U32, name="words", tag="words", align_bytes=64)
+            scales = codep.tile([P, width], U8, name="scales", tag="scales", align_bytes=64)
+            nc.vector.quantize_mx(out=words[:].bitcast(FP8X4), scales=scales[:], in_=grouped[:])
+            return words, scales
+
+        def multiply(acc, e, a, codes, c0):
+            words, scales = codes
+            slots = slice(e * C, (e + 1) * C)
+            nc.tensor.matmul_mx(out=acc, lhsT=words[:, c0:c0 + P].bitcast(FP8X4), lhsT_scale=scales[:, c0:c0 + P],
+                                rhs=s_words[a][:, slots].bitcast(FP8X4), rhs_scale=s_scales[4 * a:P, slots],
+                                start=(a == 0), stop=(a == PASSES - 1))
 
         x_raw = []
         for a in range(PASSES):
-            raw = xp.tile([P, PACK, T], F32, name="xraw", tag="xraw")
+            raw = rawp.tile([P, PACK, T], F32, name="raw", tag="x%d" % a)
             nc.sync.dma_start(out=raw[:], in_=x_view[a])
             x_raw.append(raw)
             if a == 0:
                 nc.sync.dma_start(offs_t[:], offs)
                 nc.sync.dma_start(out=gate_rows[0:T // P], in_=gate[:, 0, :].rearrange("r (q t) -> q r t", t=P))
-
-        w_raw = {}
-        fine = []
-
-        def load_group(blk, u0, units):
-            cols = slice(blk * P, (blk + 1) * P)
-            if units == 1:
-                if u0 % FINE == 0:
-                    fine.append(xp.tile([P, FINE, PACK, P], F32, name="xraw", tag="xraw"))
-                raw = fine[-1][:, u0 % FINE]
-                nc.sync.dma_start(out=raw, in_=w_view[:, :, u0, cols])
-            else:
-                raw = rawp.tile([P, PACK, units * P], F32, name="raw", tag="raw%d_%d" % (blk, u0))
-                for j in range(PACK):
-                    nc.sync.dma_start(out=raw[:, j, :].rearrange("p (u n) -> p u n", n=P), in_=w_view[:, j, u0:u0 + units, cols])
-            w_raw[(blk, u0)] = raw
-
-        def groups_of(blk):
-            if blk == BLOCKS - 1:
-                return [(0, GROUP), (GROUP, GROUP)] + [(u, 1) for u in range(2 * GROUP, UNITS)]
-            return [(u, GROUP) for u in range(0, UNITS, GROUP)]
-
-        for blk in range(BLOCKS):
-            for u0, units in groups_of(blk):
-                load_group(blk, u0, units)
-                if blk == 0 and u0 == 0:
-                    nc.sync.dma_start(out=bias_t[:], in_=b.rearrange("(c p) e -> p c e", p=P))
-            if blk == 0:
+        early_raw = {}
+        for e in range(EARLY):
+            for a in range(PASSES):
+                raw = rawp.tile([P, PACK, N], F32, name="raw", tag="w%d" % (e * PASSES + a))
+                nc.sync.dma_start(out=raw[:], in_=w_view[e, a])
+                early_raw[(e, a)] = raw
+            if e == 0:
+                nc.sync.dma_start(out=bias_t[:], in_=b.rearrange("(c p) e -> p c e", p=P))
+            if e == 1:
                 for r, pos in enumerate((pos1, pos2, pos3)):
                     nc.sync.dma_start(pos_t[r][:], pos)
 
+        def late_chunks():
+            pairs = [[(e, a) for e in range(EARLY, E)] for a in range(PASSES - 1)]
+            return pairs + [[(e, PASSES - 1)] for e in range(EARLY, E)]
+
+        late_raw = {}
+        for blk in range(BLOCKS):
+            for i, chunk in enumerate(late_chunks()):
+                raw = rawp.tile([P, PACK, len(chunk) * P], F32, name="raw", tag="late%d_%d" % (blk, i))
+                for u, (e, a) in enumerate(chunk):
+                    nc.sync.dma_start(out=raw[:, :, u * P:(u + 1) * P], in_=w_view[e, a][:, :, blk * P:(blk + 1) * P])
+                late_raw[(blk, i)] = raw
+
         nc.vector.memset(x_scales[:].bitcast(I32), 0)
-        out_t = xp.tile([P, BLOCKS, T], F32, name="xraw", tag="xraw")
         for a in range(PASSES):
             for h in range(2):
                 cols = slice(h * (T // 2), (h + 1) * (T // 2))
-                grouped = cast(a == 0 and h == 0, x_raw[a], h * (T // 2), T // 2)
+                grouped = cast(a == 0 and h == 0, x_raw[a], h * (T // 2), T // 2, bfp)
                 nc.vector.quantize_mx(out=x_words[a][:, cols].bitcast(FP8X4), scales=x_scales[4 * a:P, cols], in_=grouped[:])
             for h in range(2):
                 nc.vector.tensor_copy(s_words[a][:, h * HALF:(h + 1) * HALF],
@@ -133,52 +135,57 @@ def tile_moe_ecr_lin_relu_kernel(tc, xT, w, b, gate, offs, pos1, pos2, pos3, out
                 nc.tensor.transpose(spread[:, q * P:(q + 1) * P], gate_cols[:, r, q:q + 1].to_broadcast([P, P]), ident[:])
             nc.scalar.copy(out=gate_t[:, r, :], in_=spread[:])
 
-        def chunks_of(blk, u0, units):
-            if units == 1:
-                return [(u0, 1, False)]
-            return [(u0, 4, False), (u0 + 4, 2, u0 < 2 * GROUP)]
-
-        def experts(blk):
+        y_t = []
+        for e in range(EARLY):
             codes = {}
-            done = 0
-            sums = []
-            for u0, units in groups_of(blk):
-                for c0, cu, on_vector in chunks_of(blk, u0, units):
-                    grouped = cast(on_vector, w_raw[(blk, u0)], (c0 - u0) * P, cu * P)
-                    words = codep.tile([P, cu * P], U32, name="words", tag="words", align_bytes=64)
-                    scales = codep.tile([P, cu * P], U8, name="scales", tag="scales", align_bytes=64)
-                    nc.vector.quantize_mx(out=words[:].bitcast(FP8X4), scales=scales[:], in_=grouped[:])
-                    for u in range(c0, c0 + cu):
-                        codes[u] = (words, scales, slice((u - c0) * P, (u - c0 + 1) * P))
-                    while (done + 1) * PASSES <= c0 + cu:
-                        e = done
-                        slots = slice(e * C, (e + 1) * C)
-                        acc = psum.tile([P, C], F32, name="acc")
-                        for a in range(PASSES):
-                            wd, sc, cols = codes[e * PASSES + a]
-                            nc.tensor.matmul_mx(out=acc[:], lhsT=wd[:, cols].bitcast(FP8X4), lhsT_scale=sc[:, cols],
-                                                rhs=s_words[a][:, slots].bitcast(FP8X4), rhs_scale=s_scales[4 * a:P, slots],
-                                                start=(a == 0), stop=(a == PASSES - 1))
-                        sums.append(acc)
-                        done = done + 1
-            last = GROUP if blk == BLOCKS - 1 else 2 * GROUP
-            y = rawp.tile([P, SLOTS + PAD], F32, name="y", tag="raw%d_%d" % (blk, last))
-            nc.gpsimd.memset(y[:, SLOTS:], 0.0)
-            for e in range(E):
-                nc.scalar.activation(y[:, e * C:(e + 1) * C], sums[e][:], RELU, bias=bias_t[:, blk, e:e + 1])
-            return y
+            for a in range(PASSES):
+                for h in range(2):
+                    on_vector = h == 1 and e * PASSES + a >= VECTOR_FROM
+                    codes[(a, h)] = quantise(cast(on_vector, early_raw[(e, a)], h * (N // 2), N // 2, bfp), N // 2)
+            acc = psum.tile([P, BLOCKS, C], F32, name="acc")
+            for blk in range(BLOCKS):
+                for a in range(PASSES):
+                    multiply(acc[:, blk, :], e, a, codes[(a, blk // 2)], (blk % 2) * P)
+            if e == 0:
+                for blk in range(BLOCKS):
+                    y = rawp.tile([P, SLOTS + PAD], F32, name="y", tag=("w%d" % blk if blk < PASSES else "x1"))
+                    nc.gpsimd.memset(y[:, SLOTS:], 0.0)
+                    y_t.append(y)
+            for blk in range(BLOCKS):
+                nc.scalar.activation(y_t[blk][:, e * C:(e + 1) * C], acc[:, blk, :], RELU, bias=bias_t[:, blk, e:e + 1])
 
-        def combine(blk, y, pieces):
-            width = T // pieces
-            prods = [prodp.tile([P, T], F32, name="prod", tag="prod%d" % r) for r in range(TOP)]
-            for h in range(pieces):
-                toks = slice(h * width, (h + 1) * width)
-                for r in range(TOP):
-                    nc.vector.tensor_tensor(prods[r][:, toks], y[:].indirect(pos_t[r][:, toks.start // 16:toks.stop // 16]),
-                                            gate_t[:, r, toks], MULT)
-                nc.vector.tensor_tensor(prods[0][:, toks], prods[0][:, toks], prods[1][:, toks], ADD)
-                nc.vector.tensor_tensor(out_t[:, blk, toks], prods[0][:, toks], prods[2][:, toks], ADD)
-                nc.sync.dma_start(out=out[blk * P:(blk + 1) * P, toks], in_=out_t[:, blk, toks])
+        out_t = rawp.tile([P, BLOCKS, T], F32, name="out_t", tag="x0")
 
+        def gathers(blk, prods, toks):
+            for r in range(TOP):
+                nc.vector.tensor_tensor(prods[r][:, toks], y_t[blk][:].indirect(pos_t[r][:, toks.start // 16:toks.stop // 16]),
+                                        gate_t[:, r, toks], MULT)
+
+        def sums(blk, prods, part, toks):
+            nc.vector.tensor_tensor(part[:, toks], prods[0][:, toks], prods[1][:, toks], ADD)
+            nc.vector.tensor_tensor(out_t[:, blk, toks], part[:, toks], prods[2][:, toks], ADD)
+            nc.sync.dma_start(out=out[blk * P:(blk + 1) * P, toks], in_=out_t[:, blk, toks])
+
+        prods = None
         for blk in range(BLOCKS):
-            combine(blk, experts(blk), 2 if blk == BLOCKS - 1 else 1)
+            accs = {e: psum.tile([P, C], F32, name="acc") for e in range(EARLY, E)}
+            chunks = late_chunks()
+            for i, chunk in enumerate(chunks):
+                width = len(chunk) * P
+                pool = lastp if i == len(chunks) - 1 else bfp
+                codes = quantise(cast(False, late_raw[(blk, i)], 0, width, pool), width)
+                for u, (e, a) in enumerate(chunk):
+                    multiply(accs[e][:], e, a, codes, u * P)
+            for e in range(EARLY, E):
+                nc.scalar.activation(y_t[blk][:, e * C:(e + 1) * C], accs[e][:], RELU, bias=bias_t[:, blk, e:e + 1])
+            if blk > 0:
+                part = lastp.tile([P, T], F32, name="part", tag="grouped", align_bytes=64)
+                sums(blk - 1, prods, part, slice(0, T))
+            prods = [rawp.tile([P, T], F32, name="prod", tag="w%d" % (PASSES + r)) for r in range(TOP)]
+            if blk < BLOCKS - 1:
+                gathers(blk, prods, slice(0, T))
+        part = lastp.tile([P, T], F32, name="part", tag="grouped", align_bytes=64)
+        for h in range(2):
+            toks = slice(h * (T // 2), (h + 1) * (T // 2))
+            gathers(BLOCKS - 1, prods, toks)
+            sums(BLOCKS - 1, prods, part, toks)

@@ -25,63 +25,83 @@ P = 128
 PACK = 4
 PASSES = K // (P * PACK)
 BLOCKS = N // P
-HALF = SLOTS // 2
+PER_COLUMN = 16
+SCALE_ROWS = 4
+RUN = 4
+BIAS_ROW = 8
+ALIGN = 64
 EARLY = 4
 VECTOR_FROM = 2
+STAGE_BUFS = 8
+CODE_BUFS = 12
 
 
 def tile_moe_ecr_lin_relu_kernel(tc, xT, w, b, gate, offs, pos1, pos2, pos3, out):
     nc = tc.nc
     with ExitStack() as ctx:
         keep = ctx.enter_context(tc.tile_pool(name="keep", bufs=1))
-        rawp = ctx.enter_context(tc.tile_pool(name="rawp", bufs=1))
-        bfp = ctx.enter_context(tc.tile_pool(name="bfp", bufs=8))
-        lastp = ctx.enter_context(tc.tile_pool(name="lastp", bufs=1))
-        codep = ctx.enter_context(tc.tile_pool(name="codep", bufs=12))
+        places = ctx.enter_context(tc.tile_pool(name="places", bufs=1))
+        stages = ctx.enter_context(tc.tile_pool(name="stages", bufs=STAGE_BUFS))
+        coded = ctx.enter_context(tc.tile_pool(name="coded", bufs=CODE_BUFS))
         psum = ctx.enter_context(tc.psum_pool(name="psum", bufs=8))
+
+        def x_place(a):
+            return "x%d" % a
+
+        def w_place(e, a):
+            return "w%d" % (e * PASSES + a)
+
+        def placed(shape, dtype, name, tag):
+            return places.tile(shape, dtype, name=name, tag=tag, align_bytes=ALIGN)
+
+        def entries(list_tile, first, last):
+            return list_tile[:, first // PER_COLUMN:last // PER_COLUMN]
 
         x_view = xT.rearrange("(a p j) t -> a p j t", p=P, j=PACK)
         w_view = w.rearrange("e (a p j) n -> e a p j n", p=P, j=PACK)
 
-        offs_t = keep.tile([P, SLOTS // 16], U16, name="offs_t")
-        pos_t = [keep.tile([P, T // 16], U16, name="pos_t%d" % r) for r in range(TOP)]
+        offs_t = keep.tile([P, SLOTS // PER_COLUMN], U16, name="offs_t")
+        pos_t = [keep.tile([P, T // PER_COLUMN], U16, name="pos_t%d" % r) for r in range(TOP)]
         gate_t = keep.tile([P, TOP, T], F32, name="gate_t")
-        bias_t = keep.tile([P, BLOCKS, E], F32, name="bias_t")
-        x_words = [keep.tile([P, T], U32, name="x_words%d" % a, align_bytes=64) for a in range(PASSES)]
-        x_scales = keep.tile([P, T], U8, name="x_scales", align_bytes=64)
-        s_words = [keep.tile([P, SLOTS], U32, name="s_words%d" % a, align_bytes=64) for a in range(PASSES)]
-        s_scales = keep.tile([P, SLOTS], U8, name="s_scales", align_bytes=64)
+        bias_t = keep.tile([P, BLOCKS, BIAS_ROW], F32, name="bias_t")
+        x_words = [keep.tile([P, T], U32, name="x_words%d" % a, align_bytes=ALIGN) for a in range(PASSES)]
+        x_scales = keep.tile([P, T], U8, name="x_scales", align_bytes=ALIGN)
+        s_words = [keep.tile([P, SLOTS], U32, name="s_words%d" % a, align_bytes=ALIGN) for a in range(PASSES)]
+        s_scales = keep.tile([P, SLOTS], U8, name="s_scales", align_bytes=ALIGN)
         ident = keep.tile([P, P], F32, name="ident")
         make_identity(nc, ident[:])
-        gate_rows = bfp.tile([P, TOP, P], F32, name="gate_rows", tag="grouped", align_bytes=64)
+        gate_rows = stages.tile([P, TOP, P], F32, name="gate_rows", tag="stage", align_bytes=ALIGN)
         nc.vector.memset(gate_rows[:], 0.0)
 
-        def cast(on_vector, raw, c0, width, pool):
-            grouped = pool.tile([P, width * PACK], BF16, name="grouped", tag="grouped", align_bytes=64)
-            dst = grouped[:].rearrange("p (c i t) -> p c t i", i=4, t=PACK)
-            src = raw[:, :, c0:c0 + width].rearrange("p t (c i) -> p c t i", i=4)
+        def new_stage(width):
+            return stages.tile([P, width * PACK], BF16, name="stage", tag="stage", align_bytes=ALIGN)[:]
+
+        def cast(on_vector, raw, first, width, stage):
+            dst = stage.rearrange("p (c i j) -> p c j i", i=RUN, j=PACK)
+            src = raw[:, :, first:first + width].rearrange("p j (c i) -> p c j i", i=RUN)
             if on_vector:
                 nc.vector.tensor_copy(out=dst, in_=src)
             else:
                 nc.scalar.copy(out=dst, in_=src)
-            return grouped
 
-        def quantise(grouped, width):
-            words = codep.tile([P, width], U32, name="words", tag="words", align_bytes=64)
-            scales = codep.tile([P, width], U8, name="scales", tag="scales", align_bytes=64)
-            nc.vector.quantize_mx(out=words[:].bitcast(FP8X4), scales=scales[:], in_=grouped[:])
+        def new_words(width):
+            return coded.tile([P, width], U32, name="words", tag="words", align_bytes=ALIGN)
+
+        def quantise(stage, width, words):
+            scales = coded.tile([P, width], U8, name="scales", tag="scales", align_bytes=ALIGN)
+            nc.vector.quantize_mx(out=words[:].bitcast(FP8X4), scales=scales[:], in_=stage)
             return words, scales
 
-        def multiply(acc, e, a, codes, c0):
+        def multiply(acc, e, a, codes, first):
             words, scales = codes
             slots = slice(e * C, (e + 1) * C)
-            nc.tensor.matmul_mx(out=acc, lhsT=words[:, c0:c0 + P].bitcast(FP8X4), lhsT_scale=scales[:, c0:c0 + P],
-                                rhs=s_words[a][:, slots].bitcast(FP8X4), rhs_scale=s_scales[4 * a:P, slots],
+            nc.tensor.matmul_mx(out=acc, lhsT=words[:, first:first + P].bitcast(FP8X4), lhsT_scale=scales[:, first:first + P],
+                                rhs=s_words[a][:, slots].bitcast(FP8X4), rhs_scale=s_scales[SCALE_ROWS * a:P, slots],
                                 start=(a == 0), stop=(a == PASSES - 1))
 
         x_raw = []
         for a in range(PASSES):
-            raw = rawp.tile([P, PACK, T], F32, name="raw", tag="x%d" % a)
+            raw = placed([P, PACK, T], F32, "raw", x_place(a))
             nc.sync.dma_start(out=raw[:], in_=x_view[a])
             x_raw.append(raw)
             if a == 0:
@@ -90,102 +110,110 @@ def tile_moe_ecr_lin_relu_kernel(tc, xT, w, b, gate, offs, pos1, pos2, pos3, out
         early_raw = {}
         for e in range(EARLY):
             for a in range(PASSES):
-                raw = rawp.tile([P, PACK, N], F32, name="raw", tag="w%d" % (e * PASSES + a))
+                raw = placed([P, PACK, N], F32, "raw", w_place(e, a))
                 nc.sync.dma_start(out=raw[:], in_=w_view[e, a])
                 early_raw[(e, a)] = raw
             if e == 0:
-                nc.sync.dma_start(out=bias_t[:], in_=b.rearrange("(c p) e -> p c e", p=P))
+                nc.sync.dma_start(out=bias_t[:, :, 0:E], in_=b.rearrange("(c p) e -> p c e", p=P))
             if e == 1:
                 for r, pos in enumerate((pos1, pos2, pos3)):
                     nc.sync.dma_start(pos_t[r][:], pos)
 
-        def late_chunks():
-            pairs = [[(e, a) for e in range(EARLY, E)] for a in range(PASSES - 1)]
-            return pairs + [[(e, PASSES - 1)] for e in range(EARLY, E)]
-
+        chunks = [[(e, a) for e in range(EARLY, E)] for a in range(PASSES - 1)] + [[(e, PASSES - 1)] for e in range(EARLY, E)]
         late_raw = {}
         for blk in range(BLOCKS):
-            for i, chunk in enumerate(late_chunks()):
-                raw = rawp.tile([P, PACK, len(chunk) * P], F32, name="raw", tag="late%d_%d" % (blk, i))
+            for i, chunk in enumerate(chunks):
+                raw = places.tile([P, PACK, len(chunk) * P], F32, name="raw", tag="late%d_%d" % (blk, i))
                 for u, (e, a) in enumerate(chunk):
                     nc.sync.dma_start(out=raw[:, :, u * P:(u + 1) * P], in_=w_view[e, a][:, :, blk * P:(blk + 1) * P])
                 late_raw[(blk, i)] = raw
 
         nc.vector.memset(x_scales[:].bitcast(I32), 0)
+        slot_halves = [(0, SLOTS // 2), (SLOTS // 2, SLOTS)]
         for a in range(PASSES):
             for h in range(2):
                 cols = slice(h * (T // 2), (h + 1) * (T // 2))
-                grouped = cast(a == 0 and h == 0, x_raw[a], h * (T // 2), T // 2, bfp)
-                nc.vector.quantize_mx(out=x_words[a][:, cols].bitcast(FP8X4), scales=x_scales[4 * a:P, cols], in_=grouped[:])
-            for h in range(2):
-                nc.vector.tensor_copy(s_words[a][:, h * HALF:(h + 1) * HALF],
-                                      x_words[a][:].indirect(offs_t[:, h * (HALF // 16):(h + 1) * (HALF // 16)]))
-        for h in range(2):
-            nc.vector.tensor_copy(s_scales[:, h * HALF:(h + 1) * HALF],
-                                  x_scales[:].indirect(offs_t[:, h * (HALF // 16):(h + 1) * (HALF // 16)]))
+                stage = new_stage(T // 2)
+                cast(a == 0 and h == 0, x_raw[a], cols.start, T // 2, stage)
+                nc.vector.quantize_mx(out=x_words[a][:, cols].bitcast(FP8X4), scales=x_scales[SCALE_ROWS * a:P, cols], in_=stage)
+            for first, last in slot_halves:
+                nc.vector.tensor_copy(s_words[a][:, first:last], x_words[a][:].indirect(entries(offs_t, first, last)))
+        for first, last in slot_halves:
+            nc.vector.tensor_copy(s_scales[:, first:last], x_scales[:].indirect(entries(offs_t, first, last)))
 
-        turned = psum.tile([P, TOP, P], F32, name="acc")
+        turned = psum.tile([P, TOP, P], F32, name="bank")
         for r in range(TOP):
             nc.tensor.transpose(turned[:, r, :], gate_rows[:, r, :], ident[:])
         gate_cols = keep.tile([P, TOP, T // P], F32, name="gate_cols")
         nc.scalar.copy(out=gate_cols[:], in_=turned[:, :, 0:T // P])
         for r in range(TOP):
-            spread = psum.tile([P, T], F32, name="acc")
+            spread = psum.tile([P, T], F32, name="bank")
             for q in range(T // P):
                 nc.tensor.transpose(spread[:, q * P:(q + 1) * P], gate_cols[:, r, q:q + 1].to_broadcast([P, P]), ident[:])
             nc.scalar.copy(out=gate_t[:, r, :], in_=spread[:])
 
+        y_places = [w_place(0, a) for a in range(PASSES)] + [x_place(1)]
         y_t = []
         for e in range(EARLY):
             codes = {}
             for a in range(PASSES):
                 for h in range(2):
-                    on_vector = h == 1 and e * PASSES + a >= VECTOR_FROM
-                    codes[(a, h)] = quantise(cast(on_vector, early_raw[(e, a)], h * (N // 2), N // 2, bfp), N // 2)
-            acc = psum.tile([P, BLOCKS, C], F32, name="acc")
+                    stage = new_stage(N // 2)
+                    cast(h == 1 and e * PASSES + a >= VECTOR_FROM, early_raw[(e, a)], h * (N // 2), N // 2, stage)
+                    codes[(a, h)] = quantise(stage, N // 2, new_words(N // 2))
+            acc = psum.tile([P, BLOCKS, C], F32, name="bank")
             for blk in range(BLOCKS):
                 for a in range(PASSES):
                     multiply(acc[:, blk, :], e, a, codes[(a, blk // 2)], (blk % 2) * P)
             if e == 0:
                 for blk in range(BLOCKS):
-                    y = rawp.tile([P, SLOTS + PAD], F32, name="y", tag=("w%d" % blk if blk < PASSES else "x1"))
+                    y = placed([P, SLOTS + PAD], F32, "y", y_places[blk])
                     nc.gpsimd.memset(y[:, SLOTS:], 0.0)
                     y_t.append(y)
             for blk in range(BLOCKS):
                 nc.scalar.activation(y_t[blk][:, e * C:(e + 1) * C], acc[:, blk, :], RELU, bias=bias_t[:, blk, e:e + 1])
 
-        out_t = rawp.tile([P, BLOCKS, T], F32, name="out_t", tag="x0")
+        out_t = placed([P, BLOCKS, T], F32, "out_t", x_place(0))
 
         def gathers(blk, prods, toks):
             for r in range(TOP):
-                nc.vector.tensor_tensor(prods[r][:, toks], y_t[blk][:].indirect(pos_t[r][:, toks.start // 16:toks.stop // 16]),
+                nc.vector.tensor_tensor(prods[r][:, toks], y_t[blk][:].indirect(entries(pos_t[r], toks.start, toks.stop)),
                                         gate_t[:, r, toks], MULT)
 
-        def sums(blk, prods, part, toks):
+        def add_and_store(blk, prods, part, toks):
             nc.vector.tensor_tensor(part[:, toks], prods[0][:, toks], prods[1][:, toks], ADD)
             nc.vector.tensor_tensor(out_t[:, blk, toks], part[:, toks], prods[2][:, toks], ADD)
             nc.sync.dma_start(out=out[blk * P:(blk + 1) * P, toks], in_=out_t[:, blk, toks])
 
+        turn_places = [w_place(2, 0), w_place(2, 1)]
         prods = None
         for blk in range(BLOCKS):
-            accs = {e: psum.tile([P, C], F32, name="acc") for e in range(EARLY, E)}
-            chunks = late_chunks()
+            accs = {e: psum.tile([P, C], F32, name="bank") for e in range(EARLY, E)}
+            block_stage = placed([P, (E - EARLY) * PASSES * P * PACK], BF16, "block_stage", turn_places[blk % 2])
+            first = 0
             for i, chunk in enumerate(chunks):
                 width = len(chunk) * P
-                pool = lastp if i == len(chunks) - 1 else bfp
-                codes = quantise(cast(False, late_raw[(blk, i)], 0, width, pool), width)
+                stage = block_stage[:, first * PACK:(first + width) * PACK]
+                first = first + width
+                cast(False, late_raw[(blk, i)], 0, width, stage)
+                if i == len(chunks) - 1 and blk < BLOCKS - 1:
+                    words = placed([P, width], U32, "words", turn_places[(blk + 1) % 2])
+                else:
+                    words = new_words(width)
+                codes = quantise(stage, width, words)
                 for u, (e, a) in enumerate(chunk):
                     multiply(accs[e][:], e, a, codes, u * P)
             for e in range(EARLY, E):
                 nc.scalar.activation(y_t[blk][:, e * C:(e + 1) * C], accs[e][:], RELU, bias=bias_t[:, blk, e:e + 1])
             if blk > 0:
-                part = lastp.tile([P, T], F32, name="part", tag="grouped", align_bytes=64)
-                sums(blk - 1, prods, part, slice(0, T))
-            prods = [rawp.tile([P, T], F32, name="prod", tag="w%d" % (PASSES + r)) for r in range(TOP)]
+                part = placed([P, T], F32, "part", turn_places[blk % 2])
+                add_and_store(blk - 1, prods, part, slice(0, T))
+            prods = [placed([P, T], F32, "prod", w_place(1, r)) for r in range(TOP)]
             if blk < BLOCKS - 1:
                 gathers(blk, prods, slice(0, T))
-        part = lastp.tile([P, T], F32, name="part", tag="grouped", align_bytes=64)
+
+        part = placed([P, T], F32, "part", w_place(2, 2))
         for h in range(2):
             toks = slice(h * (T // 2), (h + 1) * (T // 2))
             gathers(BLOCKS - 1, prods, toks)
-            sums(BLOCKS - 1, prods, part, toks)
+            add_and_store(BLOCKS - 1, prods, part, toks)

from contextlib import ExitStack

import concourse.mybir as mybir
from concourse.masks import make_identity

K, T, E, C, N = 1536, 512, 6, 128, 512
TOP = 3
PAD = 64
SLOTS = E * C
FLOPS = 2 * K * N * SLOTS
BYTES = 4 * (K * T + E * K * N + N * E + TOP * T + N * T) + 2 * (SLOTS + TOP * T)

F32 = mybir.dt.float32
BF16 = mybir.dt.bfloat16
U32 = mybir.dt.uint32
I32 = mybir.dt.int32
U16 = mybir.dt.uint16
U8 = mybir.dt.uint8
FP8X4 = mybir.dt.float8_e4m3fn_x4
MULT = mybir.AluOpType.mult
ADD = mybir.AluOpType.add
RELU = mybir.ActivationFunctionType.Relu

P = 128
PACK = 4
PASSES = K // (P * PACK)
BLOCKS = N // P
PER_COLUMN = 16
SCALE_ROWS = 4
RUN = 4
BIAS_ROW = 8
ALIGN = 64
EARLY = 4
VECTOR_FROM = 2
STAGE_BUFS = 8
CODE_BUFS = 12


def tile_moe_ecr_lin_relu_kernel(tc, xT, w, b, gate, offs, pos1, pos2, pos3, out):
    nc = tc.nc
    with ExitStack() as ctx:
        keep = ctx.enter_context(tc.tile_pool(name="keep", bufs=1))
        places = ctx.enter_context(tc.tile_pool(name="places", bufs=1))
        stages = ctx.enter_context(tc.tile_pool(name="stages", bufs=STAGE_BUFS))
        coded = ctx.enter_context(tc.tile_pool(name="coded", bufs=CODE_BUFS))
        psum = ctx.enter_context(tc.psum_pool(name="psum", bufs=8))

        def x_place(a):
            return "x%d" % a

        def w_place(e, a):
            return "w%d" % (e * PASSES + a)

        def placed(shape, dtype, name, tag):
            return places.tile(shape, dtype, name=name, tag=tag, align_bytes=ALIGN)

        def entries(list_tile, first, last):
            return list_tile[:, first // PER_COLUMN:last // PER_COLUMN]

        x_view = xT.rearrange("(a p j) t -> a p j t", p=P, j=PACK)
        w_view = w.rearrange("e (a p j) n -> e a p j n", p=P, j=PACK)

        offs_t = keep.tile([P, SLOTS // PER_COLUMN], U16, name="offs_t")
        pos_t = [keep.tile([P, T // PER_COLUMN], U16, name="pos_t%d" % r) for r in range(TOP)]
        gate_t = keep.tile([P, TOP, T], F32, name="gate_t")
        bias_t = keep.tile([P, BLOCKS, BIAS_ROW], F32, name="bias_t")
        x_words = [keep.tile([P, T], U32, name="x_words%d" % a, align_bytes=ALIGN) for a in range(PASSES)]
        x_scales = keep.tile([P, T], U8, name="x_scales", align_bytes=ALIGN)
        s_words = [keep.tile([P, SLOTS], U32, name="s_words%d" % a, align_bytes=ALIGN) for a in range(PASSES)]
        s_scales = keep.tile([P, SLOTS], U8, name="s_scales", align_bytes=ALIGN)
        ident = keep.tile([P, P], F32, name="ident")
        make_identity(nc, ident[:])
        gate_rows = stages.tile([P, TOP, P], F32, name="gate_rows", tag="stage", align_bytes=ALIGN)
        nc.vector.memset(gate_rows[:], 0.0)

        def new_stage(width):
            return stages.tile([P, width * PACK], BF16, name="stage", tag="stage", align_bytes=ALIGN)[:]

        def cast(on_vector, raw, first, width, stage):
            dst = stage.rearrange("p (c i j) -> p c j i", i=RUN, j=PACK)
            src = raw[:, :, first:first + width].rearrange("p j (c i) -> p c j i", i=RUN)
            if on_vector:
                nc.vector.tensor_copy(out=dst, in_=src)
            else:
                nc.scalar.copy(out=dst, in_=src)

        def new_words(width):
            return coded.tile([P, width], U32, name="words", tag="words", align_bytes=ALIGN)

        def quantise(stage, width, words):
            scales = coded.tile([P, width], U8, name="scales", tag="scales", align_bytes=ALIGN)
            nc.vector.quantize_mx(out=words[:].bitcast(FP8X4), scales=scales[:], in_=stage)
            return words, scales

        def multiply(acc, e, a, codes, first):
            words, scales = codes
            slots = slice(e * C, (e + 1) * C)
            nc.tensor.matmul_mx(out=acc, lhsT=words[:, first:first + P].bitcast(FP8X4), lhsT_scale=scales[:, first:first + P],
                                rhs=s_words[a][:, slots].bitcast(FP8X4), rhs_scale=s_scales[SCALE_ROWS * a:P, slots],
                                start=(a == 0), stop=(a == PASSES - 1))

        x_raw = []
        for a in range(PASSES):
            raw = placed([P, PACK, T], F32, "raw", x_place(a))
            nc.sync.dma_start(out=raw[:], in_=x_view[a])
            x_raw.append(raw)
            if a == 0:
                nc.sync.dma_start(offs_t[:], offs)
                nc.sync.dma_start(out=gate_rows[0:T // P], in_=gate[:, 0, :].rearrange("r (q t) -> q r t", t=P))
        early_raw = {}
        for e in range(EARLY):
            for a in range(PASSES):
                raw = placed([P, PACK, N], F32, "raw", w_place(e, a))
                nc.sync.dma_start(out=raw[:], in_=w_view[e, a])
                early_raw[(e, a)] = raw
            if e == 0:
                nc.sync.dma_start(out=bias_t[:, :, 0:E], in_=b.rearrange("(c p) e -> p c e", p=P))
            if e == 1:
                for r, pos in enumerate((pos1, pos2, pos3)):
                    nc.sync.dma_start(pos_t[r][:], pos)

        chunks = [[(e, a) for e in range(EARLY, E)] for a in range(PASSES - 1)] + [[(e, PASSES - 1)] for e in range(EARLY, E)]
        late_raw = {}
        for blk in range(BLOCKS):
            for i, chunk in enumerate(chunks):
                raw = places.tile([P, PACK, len(chunk) * P], F32, name="raw", tag="late%d_%d" % (blk, i))
                for u, (e, a) in enumerate(chunk):
                    nc.sync.dma_start(out=raw[:, :, u * P:(u + 1) * P], in_=w_view[e, a][:, :, blk * P:(blk + 1) * P])
                late_raw[(blk, i)] = raw

        nc.vector.memset(x_scales[:].bitcast(I32), 0)
        slot_halves = [(0, SLOTS // 2), (SLOTS // 2, SLOTS)]
        for a in range(PASSES):
            for h in range(2):
                cols = slice(h * (T // 2), (h + 1) * (T // 2))
                stage = new_stage(T // 2)
                cast(a == 0 and h == 0, x_raw[a], cols.start, T // 2, stage)
                nc.vector.quantize_mx(out=x_words[a][:, cols].bitcast(FP8X4), scales=x_scales[SCALE_ROWS * a:P, cols], in_=stage)
            for first, last in slot_halves:
                nc.vector.tensor_copy(s_words[a][:, first:last], x_words[a][:].indirect(entries(offs_t, first, last)))
        for first, last in slot_halves:
            nc.vector.tensor_copy(s_scales[:, first:last], x_scales[:].indirect(entries(offs_t, first, last)))

        turned = psum.tile([P, TOP, P], F32, name="bank")
        for r in range(TOP):
            nc.tensor.transpose(turned[:, r, :], gate_rows[:, r, :], ident[:])
        gate_cols = keep.tile([P, TOP, T // P], F32, name="gate_cols")
        nc.scalar.copy(out=gate_cols[:], in_=turned[:, :, 0:T // P])
        for r in range(TOP):
            spread = psum.tile([P, T], F32, name="bank")
            for q in range(T // P):
                nc.tensor.transpose(spread[:, q * P:(q + 1) * P], gate_cols[:, r, q:q + 1].to_broadcast([P, P]), ident[:])
            nc.scalar.copy(out=gate_t[:, r, :], in_=spread[:])

        y_places = [w_place(0, a) for a in range(PASSES)] + [x_place(1)]
        y_t = []
        for e in range(EARLY):
            codes = {}
            for a in range(PASSES):
                for h in range(2):
                    stage = new_stage(N // 2)
                    cast(h == 1 and e * PASSES + a >= VECTOR_FROM, early_raw[(e, a)], h * (N // 2), N // 2, stage)
                    codes[(a, h)] = quantise(stage, N // 2, new_words(N // 2))
            acc = psum.tile([P, BLOCKS, C], F32, name="bank")
            for blk in range(BLOCKS):
                for a in range(PASSES):
                    multiply(acc[:, blk, :], e, a, codes[(a, blk // 2)], (blk % 2) * P)
            if e == 0:
                for blk in range(BLOCKS):
                    y = placed([P, SLOTS + PAD], F32, "y", y_places[blk])
                    nc.gpsimd.memset(y[:, SLOTS:], 0.0)
                    y_t.append(y)
            for blk in range(BLOCKS):
                nc.scalar.activation(y_t[blk][:, e * C:(e + 1) * C], acc[:, blk, :], RELU, bias=bias_t[:, blk, e:e + 1])

        out_t = placed([P, BLOCKS, T], F32, "out_t", x_place(0))

        def gathers(blk, prods, toks):
            for r in range(TOP):
                nc.vector.tensor_tensor(prods[r][:, toks], y_t[blk][:].indirect(entries(pos_t[r], toks.start, toks.stop)),
                                        gate_t[:, r, toks], MULT)

        def add_and_store(blk, prods, part, toks):
            nc.vector.tensor_tensor(part[:, toks], prods[0][:, toks], prods[1][:, toks], ADD)
            nc.vector.tensor_tensor(out_t[:, blk, toks], part[:, toks], prods[2][:, toks], ADD)
            nc.sync.dma_start(out=out[blk * P:(blk + 1) * P, toks], in_=out_t[:, blk, toks])

        turn_places = [w_place(2, 0), w_place(2, 1)]
        prods = None
        for blk in range(BLOCKS):
            accs = {e: psum.tile([P, C], F32, name="bank") for e in range(EARLY, E)}
            block_stage = placed([P, (E - EARLY) * PASSES * P * PACK], BF16, "block_stage", turn_places[blk % 2])
            first = 0
            for i, chunk in enumerate(chunks):
                width = len(chunk) * P
                stage = block_stage[:, first * PACK:(first + width) * PACK]
                first = first + width
                cast(False, late_raw[(blk, i)], 0, width, stage)
                if i == len(chunks) - 1 and blk < BLOCKS - 1:
                    words = placed([P, width], U32, "words", turn_places[(blk + 1) % 2])
                else:
                    words = new_words(width)
                codes = quantise(stage, width, words)
                for u, (e, a) in enumerate(chunk):
                    multiply(accs[e][:], e, a, codes, u * P)
            for e in range(EARLY, E):
                nc.scalar.activation(y_t[blk][:, e * C:(e + 1) * C], accs[e][:], RELU, bias=bias_t[:, blk, e:e + 1])
            if blk > 0:
                part = placed([P, T], F32, "part", turn_places[blk % 2])
                add_and_store(blk - 1, prods, part, slice(0, T))
            prods = [placed([P, T], F32, "prod", w_place(1, r)) for r in range(TOP)]
            if blk < BLOCKS - 1:
                gathers(blk, prods, slice(0, T))

        part = placed([P, T], F32, "part", w_place(2, 2))
        for h in range(2):
            toks = slice(h * (T // 2), (h + 1) * (T // 2))
            gathers(BLOCKS - 1, prods, toks)
            add_and_store(BLOCKS - 1, prods, part, toks)
